import numpy as np
import ml_dtypes


def mxq(x, axis, fmt="e4m3"):
    dtype, down = {"e4m3": (ml_dtypes.float8_e4m3fn, 7), "e5m2": (ml_dtypes.float8_e5m2, 14)}[fmt]
    v = np.moveaxis(np.asarray(x, np.float32).astype(ml_dtypes.bfloat16).astype(np.float64), axis, -1)
    blocks = v.reshape(v.shape[:-1] + (-1, 32))
    amax = np.abs(blocks).max(-1, keepdims=True)
    byte = np.maximum(np.where(amax > 0, np.frexp(amax)[1] - 1 + 127, 0) - down, 1)
    scale = np.exp2(byte - 127.0)
    codes = (blocks / scale).astype(np.float32).astype(dtype).astype(np.float64)
    return np.moveaxis((codes * scale).reshape(v.shape), -1, axis)


WIDE = False


def mx_kscale(k):
    if not WIDE:
        return np.ones(k)
    levels = np.array([10, -10, 5, -5, 0])
    if k % 512:
        return np.exp2(np.random.permutation(np.resize(levels, k // 32))).repeat(32)
    a = np.empty((k // 512, 16))
    for p in range(k // 512):
        a[p, :8] = np.random.permutation(np.resize(levels, 8))
        for g in range(8):
            far = levels[np.abs(levels - a[p, g]) >= 10]
            a[p, g + 8] = far[np.random.randint(len(far))]
    return np.exp2(a.ravel()).repeat(32)


def f64(x):
    return np.asarray(x).astype(np.float64)


def striped(idx):
    return np.tile(idx.reshape(-1, 16).T, (8, 1)).astype(np.uint16)


def unstriped(offs):
    return offs[:16].T.reshape(-1).astype(np.int64)


def striped8(idx):
    return np.concatenate([x.reshape(-1, 16).T for x in idx]).astype(np.uint16)


def runs(offs, k):
    lists = np.stack([offs[16 * r : 16 * r + 16].T.reshape(-1) for r in range(8)]).astype(np.int64)
    return lists[np.arange(k) % 512 // 64]


def pack_weight(w):
    k, n = w.shape
    w = f64(np.asarray(w, np.float32).astype(ml_dtypes.bfloat16)).reshape(k // 32, 32, n)
    amax = np.abs(w).max(1)
    byte = np.clip(np.where(amax > 0, np.frexp(amax)[1] - 1 + 127 - 7, 1), 1, 254)
    scaled = (w * np.exp2(127.0 - byte)[:, None, :]).reshape(k, n).astype(np.float32)
    words = np.ascontiguousarray(scaled.reshape(k // 512, 128, 4, n).transpose(0, 1, 3, 2)).astype(ml_dtypes.float8_e4m3fn).view(np.uint8)
    return words, np.ascontiguousarray(byte.astype(np.uint8).reshape(k // 512, 16, n))


def unpack_weight(words, scales):
    g, p, n, _ = words.shape
    vals = np.ascontiguousarray(words).view(ml_dtypes.float8_e4m3fn).astype(np.float64) * np.repeat(np.exp2(scales.astype(np.float64) - 127.0), 8, axis=1)[..., None]
    return vals.transpose(0, 1, 3, 2).reshape(g * 512, n)


E2M1 = np.array([0.0, 0.5, 1.0, 1.5, 2.0, 3.0, 4.0, 6.0, -0.0, -0.5, -1.0, -1.5, -2.0, -3.0, -4.0, -6.0])


def pack_fp4(w):
    k, n = w.shape
    w = f64(np.asarray(w, np.float32).astype(ml_dtypes.bfloat16)).reshape(k // 32, 32, n)
    amax = np.abs(w).max(1)
    mant, ex = np.frexp(amax / 6.0)
    byte = np.clip(np.where(amax > 0, np.where(mant > 0.5, ex, ex - 1) + 127, 1), 1, 254)
    scaled = (w * np.exp2(127.0 - byte)[:, None, :]).reshape(k, n).astype(np.float32)
    c = np.ascontiguousarray(scaled.reshape(k // 512, 128, 4, n).transpose(0, 1, 3, 2)).astype(ml_dtypes.float4_e2m1fn).view(np.uint8) & 0xF
    words = (c[..., 0::2] | (c[..., 1::2] << 4)).reshape(k // 512, 128, 2 * n)
    return np.ascontiguousarray(words), np.ascontiguousarray(byte.astype(np.uint8).reshape(k // 512, 16, n))


def unpack_fp4(words, scales):
    g, _, n = scales.shape
    words = np.ascontiguousarray(words).reshape(g, 128, n, 2)
    nib = np.empty((g, 128, n, 4), np.uint8)
    nib[..., 0::2] = words & 0xF
    nib[..., 1::2] = words >> 4
    vals = E2M1[nib] * np.repeat(np.exp2(scales.astype(np.float64) - 127.0), 8, axis=1)[..., None]
    return vals.transpose(0, 1, 3, 2).reshape(g * 512, n)


def planes(y):
    n, m = y.shape
    v = y.astype(np.float32).astype(ml_dtypes.bfloat16).astype(np.float64).reshape(n // 32, 32, m)
    top = np.abs(v).max(1)
    byte = np.clip(np.where(top > 0, np.frexp(top)[1] - 1 + 127 - 7, 1), 1, 254)
    codes = (v * np.exp2(127.0 - byte)[:, None, :]).reshape(n, m).astype(np.float32).astype(ml_dtypes.float8_e4m3fn).view(np.uint8)
    words = codes.reshape(n // 512, 128, 4, m).transpose(0, 1, 3, 2)
    return np.ascontiguousarray(words), np.ascontiguousarray(byte.astype(np.uint8).reshape(n // 512, 16, m))


K, T, S, N, H = 512, 2048, 512, 512, 512
P = 2 ** 7


def setup_inputs():
    n = np.random.standard_normal
    s = mx_kscale(K)[:, None]
    u = mx_kscale(H)
    packed_xT = pack_weight(n((K, T)) * s)
    packed_w1 = pack_fp4(n((K, H)) / np.sqrt(K) / s)
    packed_w2 = pack_fp4(n((H, H)) / np.sqrt(H) / u[:, None])
    packed_w3 = pack_fp4(n((H, N)) / np.sqrt(H) / u[:, None])
    return {
        "x_words": packed_xT[0],
        "x_scales": packed_xT[1],
        "w1_words": packed_w1[0],
        "w1_scales": packed_w1[1],
        "seed": n((H, S)).astype(np.float32),
        "kn": np.tile(np.random.uniform(0.0, 1.0, S), (P, 1)).astype(np.float32),
        "gn": (np.random.uniform(0.5, 1.5, (H, 1)) * u[:, None]).astype(np.float32),
        "w2_words": packed_w2[0],
        "w2_scales": packed_w2[1],
        "res": n((N, S)).astype(np.float32),
        "w3_words": packed_w3[0],
        "w3_scales": packed_w3[1],
        "offs": striped(np.random.permutation(T)[:S]),
        "e1": striped8(np.stack([np.random.permutation(S) for _ in range(8)])),
        "e2": striped8(np.stack([np.random.permutation(S) for _ in range(8)])),
        "mv": striped8(np.stack([np.random.permutation(S) for _ in range(8)])),
    }


def reference(x_words, x_scales, w1_words, w1_scales, seed, kn, gn, w2_words, w2_scales, res, w3_words, w3_scales, offs, e1, e2, mv):
    xq = unpack_weight(x_words, x_scales)[:, unstriped(offs)]
    y = unpack_fp4(w1_words, w1_scales).T @ xq
    v1 = 0.75 * (y[np.arange(H)[:, None], runs(e1, H)] + y[np.arange(H)[:, None], runs(e2, H)])
    z = f64(gn) * (v1 + f64(kn)[:1] * (f64(seed) - v1))
    h = np.tanh(unpack_fp4(w2_words, w2_scales).T @ mxq(z, 0, "e4m3"))
    z2 = f64(gn) * (h[np.arange(H)[:, None], runs(mv, H)])
    out_0 = f64(res) + (unpack_fp4(w3_words, w3_scales).T @ mxq(z2, 0, "e4m3"))
    return (out_0,) + planes(out_0)

@@ -1,0 +1,305 @@
+from contextlib import ExitStack
+
+import concourse.mybir as mybir
+from concourse.masks import make_identity
+
+FLOPS = 805306368
+
+F32 = mybir.dt.float32
+BF16 = mybir.dt.bfloat16
+I32 = mybir.dt.int32
+U32 = mybir.dt.uint32
+U16 = mybir.dt.uint16
+U8 = mybir.dt.uint8
+FP8X4 = mybir.dt.float8_e4m3fn_x4
+FP4X4 = mybir.dt.float4_e2m1fn_x4
+ACT = mybir.ActivationFunctionType
+ALU = mybir.AluOpType
+
+P = 128
+T = 2048
+S = 512
+HALF = 256
+CH = 128
+NCH = S // CH
+LANES = 16
+
+V_STAGE2 = [[(0, 2), (0, 3), (1, 2), (1, 3)], [(0, 2), (0, 3), (1, 2), (1, 3)], [(0, 2), (0, 3), (1, 2), (1, 3)], [(1, 2), (1, 3)]]
+V_STAGE3 = [[2, 3], [2, 3], [2, 3], []]
+V_CAST = [3]
+S_WEAVE = [3]
+
+
+def tile_picked_clampprop_none_po_kernel(
+    tc, x_words, x_scales, w1_words, w1_scales, seed, kn, gn, w2_words, w2_scales, res, w3_words, w3_scales,
+    offs, e1, e2, mv, out_0, out_1, out_2,
+):
+    nc = tc.nc
+    with ExitStack() as ctx:
+        sb = ctx.enter_context(tc.tile_pool(name="sb", bufs=1))
+        ps = ctx.enter_context(tc.psum_pool(name="ps", bufs=1))
+
+        def psum(b, shape):
+            return ps.tile(shape, F32, name="bank%d" % b)
+
+        def new(name, shape, dtype, bufs=1):
+            return sb.tile(shape, dtype, name=name, align_bytes=64, bufs=bufs)
+
+        def load_list(name, src):
+            tile = new(name, [P, S // LANES], U16)
+            nc.sync.dma_start(tile[:], src)
+            return tile
+
+        def entries(lst, start, count):
+            return lst[:, start // LANES : (start + count) // LANES]
+
+        def deal_words(name, raw, on_scalar):
+            dealt = new(name, [P, 2 * S], U8)
+            if not on_scalar:
+                nc.gpsimd.tensor_copy(
+                    out=dealt[:].rearrange("p (t m b) -> p t m b", t=4, b=2),
+                    in_=raw[:].rearrange("p (m t b) -> p t m b", t=4, b=2),
+                )
+                return dealt
+            nc.scalar.copy(
+                out=dealt[:].bitcast(U16).rearrange("p (t m) -> p t m", t=4),
+                in_=raw[:].bitcast(U16).rearrange("p (m t) -> p t m", t=4),
+            )
+            return dealt
+
+        def deal_scales(name, raw, engine):
+            dealt = new(name, [P, S], U8)
+            engine.tensor_copy(
+                out=dealt[:].rearrange("p (t m) -> p t m", t=4), in_=raw[:].rearrange("p (m t) -> p t m", t=4)
+            )
+            return dealt
+
+        def product(out, words, scales, t, codes, code_scales):
+            nc.tensor.matmul_mx(
+                out=out,
+                lhsT=words[:, 2 * P * t : 2 * P * (t + 1)].bitcast(FP4X4),
+                lhsT_scale=scales[:, P * t : P * (t + 1)],
+                rhs=codes.bitcast(FP8X4),
+                rhs_scale=code_scales,
+                start=True,
+                stop=True,
+            )
+
+        def gather(on_vector, out, window, offsets):
+            if on_vector:
+                nc.vector.tensor_copy(out=out, in_=window[:].indirect(offsets))
+            else:
+                nc.scalar.activation(out=out, in_=window[:].indirect(offsets), func=ACT.Copy)
+
+        def interleave(on_vector, out, planes):
+            dst = out[:].rearrange("p (c i t) -> p c t i", i=4, t=4)
+            src = planes[:].rearrange("p t (c i) -> p c t i", i=4)
+            if on_vector:
+                nc.vector.tensor_copy(out=dst, in_=src)
+            else:
+                nc.scalar.copy(out=dst, in_=src)
+
+        def load_rows(queue, tile, scales, quadrants):
+            for q in quadrants:
+                queue.dma_start(out=tile[32 * q : 32 * q + 4, :].bitcast(I32), in_=scales[0, 4 * q : 4 * q + 4, :].bitcast(I32))
+
+        xs_raw = new("xs_raw", [P, T], U8)
+        nc.vector.memset(xs_raw[:, 0 : T // 2].bitcast(I32), 0)
+        nc.gpsimd.memset(xs_raw[:, T // 2 : T].bitcast(I32), 0)
+        ws_raw = [new("ws_raw%d" % i, [P, S], U8) for i in range(3)]
+        for tile in ws_raw:
+            nc.gpsimd.memset(tile[:].bitcast(I32), 0)
+        ident = new("ident", [P, P], F32)
+        make_identity(nc, ident[:])
+
+        offs_sb = load_list("offs_sb", offs)
+        ww_raw = [new("ww_raw%d" % i, [P, 2 * S], U8) for i in range(3)]
+        nc.scalar.dma_start(out=ww_raw[0][:].bitcast(I32), in_=w1_words[0].bitcast(I32))
+        load_rows(nc.sync, xs_raw, x_scales, (0, 1))
+        load_rows(nc.scalar, xs_raw, x_scales, (2, 3))
+        xw_raw = new("xw_raw", [P, T], U32)
+        nc.sync.dma_start(out=xw_raw[:].bitcast(I32), in_=x_words[0].rearrange("p n t -> p (n t)").bitcast(I32))
+        load_rows(nc.scalar, ws_raw[0], w1_scales, (0, 1, 2, 3))
+        gain = new("gain", [P, 4], F32)
+        nc.scalar.dma_start(out=gain[:], in_=gn.rearrange("(p t) o -> p (t o)", t=4))
+        seed_v = seed.rearrange("(p t) j -> p t j", t=4)
+        seed_sb = [new("seed%d" % h, [P, 4, HALF], F32) for h in range(2)]
+        nc.sync.dma_start(out=seed_sb[0][:], in_=seed_v[:, :, 0:HALF])
+        known = new("known", [P, NCH], F32)
+        with nc.allow_non_contiguous_dma(reason="one value a partition and chunk"):
+            nc.scalar.dma_start(out=known[:], in_=kn[0, :].rearrange("(c p) -> p c", p=P))
+        nbr = [load_list("e1_sb", e1), load_list("e2_sb", e2)]
+        nc.sync.dma_start(out=seed_sb[1][:], in_=seed_v[:, :, HALF:S])
+        nc.sync.dma_start(out=ww_raw[1][:].bitcast(I32), in_=w2_words[0].bitcast(I32))
+        load_rows(nc.sync, ws_raw[1], w2_scales, (0, 1, 2, 3))
+        mv_sb = load_list("mv_sb", mv)
+        nc.sync.dma_start(out=ww_raw[2][:].bitcast(I32), in_=w3_words[0].bitcast(I32))
+        load_rows(nc.sync, ws_raw[2], w3_scales, (0, 1, 2, 3))
+        res_sb = new("res_sb", [P, 4, S], F32)
+        nc.sync.dma_start(out=res_sb[:], in_=res.rearrange("(p t) j -> p t j", t=4))
+
+        w1w = deal_words("w1w", ww_raw[0], True)
+        w1s = deal_scales("w1s", ws_raw[0], nc.gpsimd)
+        gain75 = new("gain75", [P, 4], F32)
+        nc.gpsimd.tensor_scalar(out=gain75[:], in0=gain[:], scalar1=0.75, scalar2=0.0, op0=ALU.mult, op1=ALU.add)
+
+        xq = [new("xq%d" % h, [P, HALF], U32) for h in range(2)]
+        xqs = [new("xqs%d" % h, [P, HALF], U8) for h in range(2)]
+        for h in range(2):
+            nc.vector.tensor_copy(out=xqs[h][:], in_=xs_raw[:].indirect(entries(offs_sb, HALF * h, HALF)))
+            nc.vector.tensor_copy(out=xq[h][:], in_=xw_raw[:].indirect(entries(offs_sb, HALF * h, HALF)))
+
+        gain_bank = psum(4, [P, 4, P])
+        for t in range(4):
+            nc.tensor.transpose(gain_bank[:, t, :], gain[:, t : t + 1].to_broadcast([P, P]), ident[:])
+        gain_row = new("gain_row", [P, 2, P, 2], F32)
+        nc.scalar.copy(out=gain_row[:], in_=gain_bank[:].rearrange("j (u e) p -> j u p e", e=2))
+        unknown = new("unknown", [P, NCH], F32)
+        nc.gpsimd.tensor_scalar(out=unknown[:], in0=known[:], scalar1=-1.0, scalar2=1.0, op0=ALU.mult, op1=ALU.add)
+
+        y = [new("y%d" % t, [P, S], F32) for t in range(4)]
+        for h in range(2):
+            for pair in range(2):
+                bank = psum(2 * h + pair, [P, 2, HALF])
+                for i in range(2):
+                    product(bank[:, i, :], w1w, w1s, 2 * pair + i, xq[h][:], xqs[h][:])
+                for i in range(2):
+                    t = 2 * pair + i
+                    dst = y[t][:, HALF * h : HALF * (h + 1)]
+                    if pair == 1:
+                        nc.vector.tensor_scalar(out=dst, in0=bank[:, i, :], scalar1=gain75[:, t : t + 1], scalar2=None, op0=ALU.mult)
+                    else:
+                        nc.scalar.activation(out=dst, in_=bank[:, i, :], func=ACT.Copy, scale=gain75[:, t : t + 1])
+
+        w2w = deal_words("w2w", ww_raw[1], False)
+        w2s = deal_scales("w2s", ws_raw[1], nc.gpsimd)
+
+        picked = [{}, {}]
+        h_raw = new("h_raw", [P, 4, S], F32)
+        hg = [new("hg%d" % t, [P, S], F32) for t in range(4)]
+        held = {}
+
+        def fetch(c):
+            for k in range(2):
+                picked[k][c] = new("picked%d" % k, [P, 4, CH], F32, bufs=4)
+            for t in range(4):
+                for k in range(2):
+                    gather((k, t) in V_STAGE2[c], picked[k][c][:, t, :], y[t], entries(nbr[k], CH * c, CH))
+
+        def known_part(c):
+            bank = psum(4 + (c + 1) % 4, [P, 4, P])
+            for t in range(4):
+                nc.tensor.transpose(bank[:, t, :], seed_sb[c // 2][:, t, CH * (c % 2) : CH * (c % 2 + 1)], ident[:])
+            for u in range(2):
+                part = new("held%d_%d" % (c, u), [P, P, 2], F32)
+                nc.vector.scalar_tensor_tensor(
+                    out=part[:], in0=bank[:, 2 * u : 2 * u + 2, :].rearrange("j e p -> j p e"), scalar=known[:, c : c + 1],
+                    in1=gain_row[:, u, :, :], op0=ALU.mult, op1=ALU.mult,
+                )
+                held[c, u] = part
+
+        def spread(c):
+            bank = psum(c, [P, 4, P])
+            for t in range(4):
+                for k in range(2):
+                    nc.tensor.matmul(bank[:, t, :], lhsT=picked[k][c][:, t, :], rhs=ident[:], is_transpose=True, start=(k == 0), stop=(k == 1))
+            back = psum(4 + (c + 1) % 4, [P, 2, P])
+            for u in range(2):
+                zt = new("zt%d_%d" % (c, u), [P, 2 * P], BF16)
+                nc.vector.scalar_tensor_tensor(
+                    out=zt[:].rearrange("j (p e) -> j p e", e=2), in0=bank[:, 2 * u : 2 * u + 2, :].rearrange("j e p -> j p e"),
+                    scalar=unknown[:, c : c + 1], in1=held[c, u][:], op0=ALU.mult, op1=ALU.add,
+                )
+                nc.tensor.transpose(back[:, u, :], zt[:].bitcast(F32), ident[:])
+            z = new("z%d" % c, [P, 4 * CH], BF16)
+            nc.scalar.copy(out=z[:].bitcast(F32).rearrange("p (j u) -> p j u", u=2), in_=back[:].rearrange("p u j -> p j u"))
+            return z
+
+        def second_product(c, z):
+            codes = new("zc%d" % c, [P, CH], U32)
+            scales = new("zs%d" % c, [P, CH], U8)
+            nc.vector.quantize_mx(out=codes[:].bitcast(FP8X4), scales=scales[:], in_=z[:])
+            if c + 1 < NCH:
+                bank = psum(c, [P, 4, CH])
+                for t in range(4):
+                    product(bank[:, t, :], w2w, w2s, t, codes[:], scales[:])
+                nc.scalar.activation(out=h_raw[:, :, CH * c : CH * (c + 1)], in_=bank[:], func=ACT.Tanh)
+                return
+            for u in (0, 1):
+                bank = psum(c - 2 * u, [P, 2, CH])
+                for e in range(2):
+                    product(bank[:, e, :], w2w, w2s, 2 * u + e, codes[:], scales[:])
+                nc.scalar.activation(out=h_raw[:, 2 * u : 2 * u + 2, CH * c : CH * (c + 1)], in_=bank[:], func=ACT.Tanh)
+
+        def apply_gain(start, stop):
+            for t in range(4):
+                nc.vector.tensor_scalar(out=hg[t][:, start:stop], in0=h_raw[:, t, start:stop], scalar1=gain[:, t : t + 1], scalar2=None, op0=ALU.mult)
+
+        for c in range(NCH):
+            fetch(c)
+        for c in range(NCH):
+            known_part(c)
+        zs = {}
+        for c in range(NCH):
+            zs[c] = spread(c)
+            if c > 0:
+                second_product(c - 1, zs[c - 1])
+        w3w = deal_words("w3w", ww_raw[2], False)
+        w3s = deal_scales("w3s", ws_raw[2], nc.gpsimd)
+        apply_gain(0, HALF)
+        apply_gain(HALF, S - CH)
+        second_product(NCH - 1, zs[NCH - 1])
+        apply_gain(S - CH, S)
+
+        out_v = out_0.rearrange("(p t) j -> p t j", t=4)
+        out_codes = new("out_codes", [P, S], U32)
+        out_scales = new("out_scales", [P, S], U8)
+        words_v = out_1[0].rearrange("p n t -> p (n t)").bitcast(I32)
+        moved = {}
+        z2 = {}
+        result = {}
+        sums = {}
+
+        def move(c):
+            moved[c] = new("moved", [P, 4, CH], BF16, bufs=4)
+            for t in range(4):
+                gather(t in V_STAGE3[c], moved[c][:, t, :], hg[t], entries(mv_sb, CH * c, CH))
+
+        def weave(c):
+            z2[c] = new("z2_%d" % c, [P, 4 * CH], BF16)
+            interleave(c not in S_WEAVE, z2[c], moved[c])
+
+        def third_product(c):
+            codes = new("z2c%d" % c, [P, CH], U32)
+            scales = new("z2s%d" % c, [P, CH], U8)
+            nc.vector.quantize_mx(out=codes[:].bitcast(FP8X4), scales=scales[:], in_=z2[c][:])
+            bank = psum(4 + (c + 1) % 4, [P, 4, CH])
+            for t in range(4):
+                product(bank[:, t, :], w3w, w3s, t, codes[:], scales[:])
+            sums[c] = bank
+
+        def add_residual(c):
+            bank = sums[c]
+            result[c] = new("result%d" % c, [P, 4, CH], F32)
+            nc.vector.tensor_tensor(out=result[c][:], in0=bank[:], in1=res_sb[:, :, CH * c : CH * (c + 1)], op=ALU.add)
+            nc.sync.dma_start(out=out_v[:, :, CH * c : CH * (c + 1)], in_=result[c][:])
+
+        def hand_on(c):
+            rounded = new("rounded%d" % c, [P, 4 * CH], BF16)
+            interleave(c in V_CAST, rounded, result[c])
+            cols = slice(CH * c, CH * (c + 1))
+            nc.vector.quantize_mx(out=out_codes[:, cols].bitcast(FP8X4), scales=out_scales[:, cols], in_=rounded[:])
+            nc.sync.dma_start(out=words_v[:, cols], in_=out_codes[:, cols].bitcast(I32))
+
+        for c in range(NCH + 2):
+            if c < NCH:
+                move(c)
+                weave(c)
+                third_product(c)
+            if 1 <= c <= NCH:
+                add_residual(c - 1)
+            if c >= 2:
+                hand_on(c - 2)
+        for q in range(4):
+            queue = nc.sync if q % 2 == 0 else nc.scalar
+            queue.dma_start(out=out_2[0, 4 * q : 4 * q + 4, :].bitcast(I32), in_=out_scales[32 * q : 32 * q + 4, :].bitcast(I32))

@@ -114,34 +114,34 @@ def tile_picked_clampprop_none_po_kernel(
 
         offs_sb = load_list("offs_sb", offs)
         ww_raw = [new("ww_raw%d" % i, [P, 2 * S], U8) for i in range(3)]
-        nc.scalar.dma_start(out=ww_raw[0][:].bitcast(I32), in_=w1_words[0].bitcast(I32))
-        load_rows(nc.sync, xs_raw, x_scales, (0, 1))
-        load_rows(nc.scalar, xs_raw, x_scales, (2, 3))
         xw_raw = new("xw_raw", [P, T], U32)
-        nc.sync.dma_start(out=xw_raw[:].bitcast(I32), in_=x_words[0].rearrange("p n t -> p (n t)").bitcast(I32))
-        load_rows(nc.scalar, ws_raw[0], w1_scales, (0, 1, 2, 3))
         gain = new("gain", [P, 4], F32)
-        nc.scalar.dma_start(out=gain[:], in_=gn.rearrange("(p t) o -> p (t o)", t=4))
         seed_v = seed.rearrange("(p t) j -> p t j", t=4)
         seed_sb = [new("seed%d" % h, [P, 4, HALF], F32) for h in range(2)]
-        nc.sync.dma_start(out=seed_sb[0][:], in_=seed_v[:, :, 0:HALF])
         known = new("known", [P, NCH], F32)
+        res_sb = new("res_sb", [P, 4, S], F32)
+        nc.scalar.dma_start(out=gain[:], in_=gn.rearrange("(p t) o -> p (t o)", t=4))
+        load_rows(nc.sync, xs_raw, x_scales, (0, 1))
+        load_rows(nc.scalar, xs_raw, x_scales, (2, 3))
+        nc.sync.dma_start(out=xw_raw[:].bitcast(I32), in_=x_words[0].rearrange("p n t -> p (n t)").bitcast(I32))
+        nc.sync.dma_start(out=ww_raw[0][:].bitcast(I32), in_=w1_words[0].bitcast(I32))
+        load_rows(nc.scalar, ws_raw[0], w1_scales, (0, 1, 2, 3))
         with nc.allow_non_contiguous_dma(reason="one value a partition and chunk"):
             nc.scalar.dma_start(out=known[:], in_=kn[0, :].rearrange("(c p) -> p c", p=P))
-        nbr = [load_list("e1_sb", e1), load_list("e2_sb", e2)]
-        nc.sync.dma_start(out=seed_sb[1][:], in_=seed_v[:, :, HALF:S])
         nc.sync.dma_start(out=ww_raw[1][:].bitcast(I32), in_=w2_words[0].bitcast(I32))
+        nbr = [load_list("e1_sb", e1), load_list("e2_sb", e2)]
+        nc.sync.dma_start(out=ww_raw[2][:].bitcast(I32), in_=w3_words[0].bitcast(I32))
+        nc.sync.dma_start(out=seed_sb[0][:], in_=seed_v[:, :, 0:HALF])
+        nc.sync.dma_start(out=seed_sb[1][:], in_=seed_v[:, :, HALF:S])
         load_rows(nc.sync, ws_raw[1], w2_scales, (0, 1, 2, 3))
         mv_sb = load_list("mv_sb", mv)
-        nc.sync.dma_start(out=ww_raw[2][:].bitcast(I32), in_=w3_words[0].bitcast(I32))
         load_rows(nc.sync, ws_raw[2], w3_scales, (0, 1, 2, 3))
-        res_sb = new("res_sb", [P, 4, S], F32)
         nc.sync.dma_start(out=res_sb[:], in_=res.rearrange("(p t) j -> p t j", t=4))
 
         w1w = deal_words("w1w", ww_raw[0], True)
-        w1s = deal_scales("w1s", ws_raw[0], nc.gpsimd)
+        w1s = deal_scales("w1s", ws_raw[0], nc.vector)
         gain75 = new("gain75", [P, 4], F32)
-        nc.gpsimd.tensor_scalar(out=gain75[:], in0=gain[:], scalar1=0.75, scalar2=0.0, op0=ALU.mult, op1=ALU.add)
+        nc.scalar.activation(out=gain75[:], in_=gain[:], func=ACT.Copy, scale=0.75)
 
         xq = [new("xq%d" % h, [P, HALF], U32) for h in range(2)]
         xqs = [new("xqs%d" % h, [P, HALF], U8) for h in range(2)]
@@ -149,30 +149,27 @@ def tile_picked_clampprop_none_po_kernel(
             nc.vector.tensor_copy(out=xqs[h][:], in_=xs_raw[:].indirect(entries(offs_sb, HALF * h, HALF)))
             nc.vector.tensor_copy(out=xq[h][:], in_=xw_raw[:].indirect(entries(offs_sb, HALF * h, HALF)))
 
-        gain_bank = psum(4, [P, 4, P])
+        gain_bank = psum(3, [P, 4, P])
         for t in range(4):
             nc.tensor.transpose(gain_bank[:, t, :], gain[:, t : t + 1].to_broadcast([P, P]), ident[:])
         gain_row = new("gain_row", [P, 2, P, 2], F32)
         nc.scalar.copy(out=gain_row[:], in_=gain_bank[:].rearrange("j (u e) p -> j u p e", e=2))
         unknown = new("unknown", [P, NCH], F32)
-        nc.gpsimd.tensor_scalar(out=unknown[:], in0=known[:], scalar1=-1.0, scalar2=1.0, op0=ALU.mult, op1=ALU.add)
+        nc.vector.tensor_scalar(out=unknown[:], in0=known[:], scalar1=-1.0, scalar2=1.0, op0=ALU.mult, op1=ALU.add)
 
         y = [new("y%d" % t, [P, S], F32) for t in range(4)]
         for h in range(2):
-            for pair in range(2):
-                bank = psum(2 * h + pair, [P, 2, HALF])
-                for i in range(2):
-                    product(bank[:, i, :], w1w, w1s, 2 * pair + i, xq[h][:], xqs[h][:])
-                for i in range(2):
-                    t = 2 * pair + i
-                    dst = y[t][:, HALF * h : HALF * (h + 1)]
-                    if pair == 1:
-                        nc.vector.tensor_scalar(out=dst, in0=bank[:, i, :], scalar1=gain75[:, t : t + 1], scalar2=None, op0=ALU.mult)
-                    else:
-                        nc.scalar.activation(out=dst, in_=bank[:, i, :], func=ACT.Copy, scale=gain75[:, t : t + 1])
+            for t in (0, 2, 1, 3):
+                bank = psum(4 * (1 - h) + t, [P, HALF])
+                product(bank[:], w1w, w1s, t, xq[h][:], xqs[h][:])
+                dst = y[t][:, HALF * h : HALF * (h + 1)]
+                if t >= 2:
+                    nc.vector.tensor_scalar(out=dst, in0=bank[:], scalar1=gain75[:, t : t + 1], scalar2=None, op0=ALU.mult)
+                else:
+                    nc.scalar.activation(out=dst, in_=bank[:], func=ACT.Copy, scale=gain75[:, t : t + 1])
 
-        w2w = deal_words("w2w", ww_raw[1], False)
-        w2s = deal_scales("w2s", ws_raw[1], nc.gpsimd)
+        w2w = deal_words("w2w", ww_raw[1], True)
+        w2s = deal_scales("w2s", ws_raw[1], nc.vector)
 
         picked = [{}, {}]
         h_raw = new("h_raw", [P, 4, S], F32)
@@ -198,11 +195,17 @@ def tile_picked_clampprop_none_po_kernel(
                 )
                 held[c, u] = part
 
-        def spread(c):
+        turned = {}
+
+        def turn(c):
             bank = psum(c, [P, 4, P])
+            turned[c] = bank
             for t in range(4):
                 for k in range(2):
                     nc.tensor.matmul(bank[:, t, :], lhsT=picked[k][c][:, t, :], rhs=ident[:], is_transpose=True, start=(k == 0), stop=(k == 1))
+
+        def spread(c):
+            bank = turned[c]
             back = psum(4 + (c + 1) % 4, [P, 2, P])
             for u in range(2):
                 zt = new("zt%d_%d" % (c, u), [P, 2 * P], BF16)
@@ -212,7 +215,8 @@ def tile_picked_clampprop_none_po_kernel(
                 )
                 nc.tensor.transpose(back[:, u, :], zt[:].bitcast(F32), ident[:])
             z = new("z%d" % c, [P, 4 * CH], BF16)
-            nc.scalar.copy(out=z[:].bitcast(F32).rearrange("p (j u) -> p j u", u=2), in_=back[:].rearrange("p u j -> p j u"))
+            copy = nc.vector.tensor_copy if c in [] else nc.scalar.copy
+            copy(out=z[:].bitcast(F32).rearrange("p (j u) -> p j u", u=2), in_=back[:].rearrange("p u j -> p j u"))
             return z
 
         def second_product(c, z):
@@ -235,20 +239,31 @@ def tile_picked_clampprop_none_po_kernel(
             for t in range(4):
                 nc.vector.tensor_scalar(out=hg[t][:, start:stop], in0=h_raw[:, t, start:stop], scalar1=gain[:, t : t + 1], scalar2=None, op0=ALU.mult)
 
-        for c in range(NCH):
-            fetch(c)
-        for c in range(NCH):
-            known_part(c)
         zs = {}
-        for c in range(NCH):
-            zs[c] = spread(c)
-            if c > 0:
-                second_product(c - 1, zs[c - 1])
-        w3w = deal_words("w3w", ww_raw[2], False)
-        w3s = deal_scales("w3s", ws_raw[2], nc.gpsimd)
+        fetch(0)
+        fetch(1)
+        fetch(2)
+        fetch(3)
+        known_part(0)
+        known_part(1)
+        known_part(2)
+        known_part(3)
+        turn(0)
+        turn(1)
+        turn(2)
+        turn(3)
+        zs[0] = spread(0)
+        zs[1] = spread(1)
+        second_product(0, zs[0])
+        zs[2] = spread(2)
+        second_product(1, zs[1])
+        zs[3] = spread(3)
+        second_product(2, zs[2])
+        w3w = deal_words("w3w", ww_raw[2], True)
+        w3s = deal_scales("w3s", ws_raw[2], nc.vector)
         apply_gain(0, HALF)
         apply_gain(HALF, S - CH)
-        second_product(NCH - 1, zs[NCH - 1])
+        second_product(3, zs[3])
         apply_gain(S - CH, S)
 
         out_v = out_0.rearrange("(p t) j -> p t j", t=4)
@@ -284,22 +299,44 @@ def tile_picked_clampprop_none_po_kernel(
             nc.vector.tensor_tensor(out=result[c][:], in0=bank[:], in1=res_sb[:, :, CH * c : CH * (c + 1)], op=ALU.add)
             nc.sync.dma_start(out=out_v[:, :, CH * c : CH * (c + 1)], in_=result[c][:])
 
+        rounds = {}
+
+        def round_out(c):
+            rounds[c] = new("rounded%d" % c, [P, 4 * CH], BF16)
+            interleave(c in V_CAST, rounds[c], result[c])
+
         def hand_on(c):
-            rounded = new("rounded%d" % c, [P, 4 * CH], BF16)
-            interleave(c in V_CAST, rounded, result[c])
+            rounded = rounds[c]
             cols = slice(CH * c, CH * (c + 1))
             nc.vector.quantize_mx(out=out_codes[:, cols].bitcast(FP8X4), scales=out_scales[:, cols], in_=rounded[:])
-            nc.sync.dma_start(out=words_v[:, cols], in_=out_codes[:, cols].bitcast(I32))
+            if c >= NCH - 2:
+                cols = slice(0 if c == NCH - 2 else CH * c, CH * (c + 1))
+                nc.sync.dma_start(out=words_v[:, cols], in_=out_codes[:, cols].bitcast(I32))
 
-        for c in range(NCH + 2):
-            if c < NCH:
-                move(c)
-                weave(c)
-                third_product(c)
-            if 1 <= c <= NCH:
-                add_residual(c - 1)
-            if c >= 2:
-                hand_on(c - 2)
+        move(0)
+        move(1)
+        move(2)
+        move(3)
+        weave(0)
+        third_product(0)
+        weave(1)
+        third_product(1)
+        add_residual(0)
+        weave(2)
+        third_product(2)
+        add_residual(1)
+        weave(3)
+        third_product(3)
+        add_residual(2)
+        add_residual(3)
+        round_out(0)
+        round_out(1)
+        round_out(2)
+        round_out(3)
+        hand_on(0)
+        hand_on(1)
+        hand_on(2)
+        hand_on(3)
         for q in range(4):
             queue = nc.sync if q % 2 == 0 else nc.scalar
             queue.dma_start(out=out_2[0, 4 * q : 4 * q + 4, :].bitcast(I32), in_=out_scales[32 * q : 32 * q + 4, :].bitcast(I32))

@@ -24,7 +24,7 @@ CH = 128
 NCH = S // CH
 LANES = 16
 
-V_STAGE2 = [[(0, 2), (0, 3), (1, 2), (1, 3)], [(0, 2), (0, 3), (1, 2), (1, 3)], [(0, 2), (0, 3), (1, 2), (1, 3)], [(1, 2), (1, 3)]]
+V_STAGE2 = [[(0, 2), (0, 3), (1, 2), (1, 3), (1, 1)], [(0, 2), (0, 3), (1, 2), (1, 3), (1, 1)], [(0, 2), (0, 3), (1, 2), (1, 3)], [(0, 2), (0, 3), (1, 2), (1, 3)]]
 V_STAGE3 = [[2, 3], [2, 3], [2, 3], []]
 V_CAST = [3]
 S_WEAVE = [3]
@@ -107,10 +107,10 @@ def tile_picked_clampprop_none_po_kernel(
         nc.vector.memset(xs_raw[:, 0 : T // 2].bitcast(I32), 0)
         nc.gpsimd.memset(xs_raw[:, T // 2 : T].bitcast(I32), 0)
         ws_raw = [new("ws_raw%d" % i, [P, S], U8) for i in range(3)]
-        for tile in ws_raw:
-            nc.gpsimd.memset(tile[:].bitcast(I32), 0)
         ident = new("ident", [P, P], F32)
         make_identity(nc, ident[:])
+        for tile in ws_raw:
+            nc.vector.memset(tile[:].bitcast(I32), 0)
 
         offs_sb = load_list("offs_sb", offs)
         ww_raw = [new("ww_raw%d" % i, [P, 2 * S], U8) for i in range(3)]
@@ -120,26 +120,26 @@ def tile_picked_clampprop_none_po_kernel(
         seed_sb = [new("seed%d" % h, [P, 4, HALF], F32) for h in range(2)]
         known = new("known", [P, NCH], F32)
         res_sb = new("res_sb", [P, 4, S], F32)
-        nc.scalar.dma_start(out=gain[:], in_=gn.rearrange("(p t) o -> p (t o)", t=4))
+        nc.scalar.dma_start(out=ww_raw[0][:].bitcast(I32), in_=w1_words[0].bitcast(I32))
         load_rows(nc.sync, xs_raw, x_scales, (0, 1))
         load_rows(nc.scalar, xs_raw, x_scales, (2, 3))
         nc.sync.dma_start(out=xw_raw[:].bitcast(I32), in_=x_words[0].rearrange("p n t -> p (n t)").bitcast(I32))
-        nc.sync.dma_start(out=ww_raw[0][:].bitcast(I32), in_=w1_words[0].bitcast(I32))
         load_rows(nc.scalar, ws_raw[0], w1_scales, (0, 1, 2, 3))
-        with nc.allow_non_contiguous_dma(reason="one value a partition and chunk"):
-            nc.scalar.dma_start(out=known[:], in_=kn[0, :].rearrange("(c p) -> p c", p=P))
-        nc.sync.dma_start(out=ww_raw[1][:].bitcast(I32), in_=w2_words[0].bitcast(I32))
-        nbr = [load_list("e1_sb", e1), load_list("e2_sb", e2)]
-        nc.sync.dma_start(out=ww_raw[2][:].bitcast(I32), in_=w3_words[0].bitcast(I32))
+        nc.scalar.dma_start(out=gain[:], in_=gn.rearrange("(p t) o -> p (t o)", t=4))
         nc.sync.dma_start(out=seed_sb[0][:], in_=seed_v[:, :, 0:HALF])
+        nbr = [load_list("e1_sb", e1), load_list("e2_sb", e2)]
         nc.sync.dma_start(out=seed_sb[1][:], in_=seed_v[:, :, HALF:S])
+        with nc.allow_non_contiguous_dma(reason="one value a partition and chunk"):
+            nc.sync.dma_start(out=known[:], in_=kn[0, :].rearrange("(c p) -> p c", p=P))
+        nc.sync.dma_start(out=ww_raw[1][:].bitcast(I32), in_=w2_words[0].bitcast(I32))
         load_rows(nc.sync, ws_raw[1], w2_scales, (0, 1, 2, 3))
+        nc.sync.dma_start(out=ww_raw[2][:].bitcast(I32), in_=w3_words[0].bitcast(I32))
         mv_sb = load_list("mv_sb", mv)
         load_rows(nc.sync, ws_raw[2], w3_scales, (0, 1, 2, 3))
         nc.sync.dma_start(out=res_sb[:], in_=res.rearrange("(p t) j -> p t j", t=4))
 
         w1w = deal_words("w1w", ww_raw[0], True)
-        w1s = deal_scales("w1s", ws_raw[0], nc.vector)
+        w1s = deal_scales("w1s", ws_raw[0], nc.gpsimd)
         gain75 = new("gain75", [P, 4], F32)
         nc.scalar.activation(out=gain75[:], in_=gain[:], func=ACT.Copy, scale=0.75)
 
@@ -149,11 +149,6 @@ def tile_picked_clampprop_none_po_kernel(
             nc.vector.tensor_copy(out=xqs[h][:], in_=xs_raw[:].indirect(entries(offs_sb, HALF * h, HALF)))
             nc.vector.tensor_copy(out=xq[h][:], in_=xw_raw[:].indirect(entries(offs_sb, HALF * h, HALF)))
 
-        gain_bank = psum(3, [P, 4, P])
-        for t in range(4):
-            nc.tensor.transpose(gain_bank[:, t, :], gain[:, t : t + 1].to_broadcast([P, P]), ident[:])
-        gain_row = new("gain_row", [P, 2, P, 2], F32)
-        nc.scalar.copy(out=gain_row[:], in_=gain_bank[:].rearrange("j (u e) p -> j u p e", e=2))
         unknown = new("unknown", [P, NCH], F32)
         nc.vector.tensor_scalar(out=unknown[:], in0=known[:], scalar1=-1.0, scalar2=1.0, op0=ALU.mult, op1=ALU.add)
 
@@ -168,8 +163,6 @@ def tile_picked_clampprop_none_po_kernel(
                 else:
                     nc.scalar.activation(out=dst, in_=bank[:], func=ACT.Copy, scale=gain75[:, t : t + 1])
 
-        w2w = deal_words("w2w", ww_raw[1], True)
-        w2s = deal_scales("w2s", ws_raw[1], nc.vector)
 
         picked = [{}, {}]
         h_raw = new("h_raw", [P, 4, S], F32)
@@ -183,17 +176,19 @@ def tile_picked_clampprop_none_po_kernel(
                 for k in range(2):
                     gather((k, t) in V_STAGE2[c], picked[k][c][:, t, :], y[t], entries(nbr[k], CH * c, CH))
 
+        def scale_seed(h):
+            for t in range(4):
+                nc.gpsimd.tensor_scalar(
+                    out=seed_gain[h][:, t, :], in0=seed_sb[h][:, t, :], scalar1=gain[:, t : t + 1], scalar2=0.0, op0=ALU.mult, op1=ALU.add
+                )
+
         def known_part(c):
             bank = psum(4 + (c + 1) % 4, [P, 4, P])
             for t in range(4):
-                nc.tensor.transpose(bank[:, t, :], seed_sb[c // 2][:, t, CH * (c % 2) : CH * (c % 2 + 1)], ident[:])
-            for u in range(2):
-                part = new("held%d_%d" % (c, u), [P, P, 2], F32)
-                nc.vector.scalar_tensor_tensor(
-                    out=part[:], in0=bank[:, 2 * u : 2 * u + 2, :].rearrange("j e p -> j p e"), scalar=known[:, c : c + 1],
-                    in1=gain_row[:, u, :, :], op0=ALU.mult, op1=ALU.mult,
-                )
-                held[c, u] = part
+                nc.tensor.transpose(bank[:, t, :], seed_gain[c // 2][:, t, CH * (c % 2) : CH * (c % 2 + 1)], ident[:])
+            part = new("held%d" % c, [P, 2, P, 2], F32)
+            nc.scalar.activation(out=part[:], in_=bank[:].rearrange("j (u e) p -> j u p e", e=2), func=ACT.Copy, scale=known[:, c : c + 1])
+            held[c] = part
 
         turned = {}
 
@@ -211,7 +206,7 @@ def tile_picked_clampprop_none_po_kernel(
                 zt = new("zt%d_%d" % (c, u), [P, 2 * P], BF16)
                 nc.vector.scalar_tensor_tensor(
                     out=zt[:].rearrange("j (p e) -> j p e", e=2), in0=bank[:, 2 * u : 2 * u + 2, :].rearrange("j e p -> j p e"),
-                    scalar=unknown[:, c : c + 1], in1=held[c, u][:], op0=ALU.mult, op1=ALU.add,
+                    scalar=unknown[:, c : c + 1], in1=held[c][:, u, :, :], op0=ALU.mult, op1=ALU.add,
                 )
                 nc.tensor.transpose(back[:, u, :], zt[:].bitcast(F32), ident[:])
             z = new("z%d" % c, [P, 4 * CH], BF16)
@@ -230,7 +225,7 @@ def tile_picked_clampprop_none_po_kernel(
                 nc.scalar.activation(out=h_raw[:, :, CH * c : CH * (c + 1)], in_=bank[:], func=ACT.Tanh)
                 return
             for u in (0, 1):
-                bank = psum(c - 2 * u, [P, 2, CH])
+                bank = psum(3 + 2 * u, [P, 2, CH])
                 for e in range(2):
                     product(bank[:, e, :], w2w, w2s, 2 * u + e, codes[:], scales[:])
                 nc.scalar.activation(out=h_raw[:, 2 * u : 2 * u + 2, CH * c : CH * (c + 1)], in_=bank[:], func=ACT.Tanh)
@@ -240,6 +235,11 @@ def tile_picked_clampprop_none_po_kernel(
                 nc.vector.tensor_scalar(out=hg[t][:, start:stop], in0=h_raw[:, t, start:stop], scalar1=gain[:, t : t + 1], scalar2=None, op0=ALU.mult)
 
         zs = {}
+        seed_gain = [new("seed_gain%d" % h, [P, 4, HALF], F32) for h in range(2)]
+        scale_seed(0)
+        scale_seed(1)
+        w2w = deal_words("w2w", ww_raw[1], False)
+        w2s = deal_scales("w2s", ws_raw[1], nc.gpsimd)
         fetch(0)
         fetch(1)
         fetch(2)
@@ -259,8 +259,8 @@ def tile_picked_clampprop_none_po_kernel(
         second_product(1, zs[1])
         zs[3] = spread(3)
         second_product(2, zs[2])
-        w3w = deal_words("w3w", ww_raw[2], True)
-        w3s = deal_scales("w3s", ws_raw[2], nc.vector)
+        w3w = deal_words("w3w", ww_raw[2], False)
+        w3s = deal_scales("w3s", ws_raw[2], nc.gpsimd)
         apply_gain(0, HALF)
         apply_gain(HALF, S - CH)
         second_product(3, zs[3])
@@ -309,8 +309,8 @@ def tile_picked_clampprop_none_po_kernel(
             rounded = rounds[c]
             cols = slice(CH * c, CH * (c + 1))
             nc.vector.quantize_mx(out=out_codes[:, cols].bitcast(FP8X4), scales=out_scales[:, cols], in_=rounded[:])
-            if c >= NCH - 2:
-                cols = slice(0 if c == NCH - 2 else CH * c, CH * (c + 1))
+            if c % 2 == 1:
+                cols = slice(CH * (c - 1), CH * (c + 1))
                 nc.sync.dma_start(out=words_v[:, cols], in_=out_codes[:, cols].bitcast(I32))
 
         move(0)

from contextlib import ExitStack

import concourse.mybir as mybir
from concourse.masks import make_identity

FLOPS = 805306368

F32 = mybir.dt.float32
BF16 = mybir.dt.bfloat16
I32 = mybir.dt.int32
U32 = mybir.dt.uint32
U16 = mybir.dt.uint16
U8 = mybir.dt.uint8
FP8X4 = mybir.dt.float8_e4m3fn_x4
FP4X4 = mybir.dt.float4_e2m1fn_x4
ACT = mybir.ActivationFunctionType
ALU = mybir.AluOpType

P = 128
T = 2048
S = 512
HALF = 256
CH = 128
NCH = S // CH
LANES = 16

V_STAGE2 = [[(0, 2), (0, 3), (1, 2), (1, 3), (1, 1)], [(0, 2), (0, 3), (1, 2), (1, 3), (1, 1)], [(0, 2), (0, 3), (1, 2), (1, 3)], [(0, 2), (0, 3), (1, 2), (1, 3)]]
V_STAGE3 = [[2, 3], [2, 3], [2, 3], []]
V_CAST = [3]
S_WEAVE = [3]


def tile_picked_clampprop_none_po_kernel(
    tc, x_words, x_scales, w1_words, w1_scales, seed, kn, gn, w2_words, w2_scales, res, w3_words, w3_scales,
    offs, e1, e2, mv, out_0, out_1, out_2,
):
    nc = tc.nc
    with ExitStack() as ctx:
        sb = ctx.enter_context(tc.tile_pool(name="sb", bufs=1))
        ps = ctx.enter_context(tc.psum_pool(name="ps", bufs=1))

        def psum(b, shape):
            return ps.tile(shape, F32, name="bank%d" % b)

        def new(name, shape, dtype, bufs=1):
            return sb.tile(shape, dtype, name=name, align_bytes=64, bufs=bufs)

        def load_list(name, src):
            tile = new(name, [P, S // LANES], U16)
            nc.sync.dma_start(tile[:], src)
            return tile

        def entries(lst, start, count):
            return lst[:, start // LANES : (start + count) // LANES]

        def deal_words(name, raw, on_scalar):
            dealt = new(name, [P, 2 * S], U8)
            if not on_scalar:
                nc.gpsimd.tensor_copy(
                    out=dealt[:].rearrange("p (t m b) -> p t m b", t=4, b=2),
                    in_=raw[:].rearrange("p (m t b) -> p t m b", t=4, b=2),
                )
                return dealt
            nc.scalar.copy(
                out=dealt[:].bitcast(U16).rearrange("p (t m) -> p t m", t=4),
                in_=raw[:].bitcast(U16).rearrange("p (m t) -> p t m", t=4),
            )
            return dealt

        def deal_scales(name, raw, engine):
            dealt = new(name, [P, S], U8)
            engine.tensor_copy(
                out=dealt[:].rearrange("p (t m) -> p t m", t=4), in_=raw[:].rearrange("p (m t) -> p t m", t=4)
            )
            return dealt

        def product(out, words, scales, t, codes, code_scales):
            nc.tensor.matmul_mx(
                out=out,
                lhsT=words[:, 2 * P * t : 2 * P * (t + 1)].bitcast(FP4X4),
                lhsT_scale=scales[:, P * t : P * (t + 1)],
                rhs=codes.bitcast(FP8X4),
                rhs_scale=code_scales,
                start=True,
                stop=True,
            )

        def gather(on_vector, out, window, offsets):
            if on_vector:
                nc.vector.tensor_copy(out=out, in_=window[:].indirect(offsets))
            else:
                nc.scalar.activation(out=out, in_=window[:].indirect(offsets), func=ACT.Copy)

        def interleave(on_vector, out, planes):
            dst = out[:].rearrange("p (c i t) -> p c t i", i=4, t=4)
            src = planes[:].rearrange("p t (c i) -> p c t i", i=4)
            if on_vector:
                nc.vector.tensor_copy(out=dst, in_=src)
            else:
                nc.scalar.copy(out=dst, in_=src)

        def load_rows(queue, tile, scales, quadrants):
            for q in quadrants:
                queue.dma_start(out=tile[32 * q : 32 * q + 4, :].bitcast(I32), in_=scales[0, 4 * q : 4 * q + 4, :].bitcast(I32))

        xs_raw = new("xs_raw", [P, T], U8)
        nc.vector.memset(xs_raw[:, 0 : T // 2].bitcast(I32), 0)
        nc.gpsimd.memset(xs_raw[:, T // 2 : T].bitcast(I32), 0)
        ws_raw = [new("ws_raw%d" % i, [P, S], U8) for i in range(3)]
        ident = new("ident", [P, P], F32)
        make_identity(nc, ident[:])
        for tile in ws_raw:
            nc.vector.memset(tile[:].bitcast(I32), 0)

        offs_sb = load_list("offs_sb", offs)
        ww_raw = [new("ww_raw%d" % i, [P, 2 * S], U8) for i in range(3)]
        xw_raw = new("xw_raw", [P, T], U32)
        gain = new("gain", [P, 4], F32)
        seed_v = seed.rearrange("(p t) j -> p t j", t=4)
        seed_sb = [new("seed%d" % h, [P, 4, HALF], F32) for h in range(2)]
        known = new("known", [P, NCH], F32)
        res_sb = new("res_sb", [P, 4, S], F32)
        nc.scalar.dma_start(out=ww_raw[0][:].bitcast(I32), in_=w1_words[0].bitcast(I32))
        load_rows(nc.sync, xs_raw, x_scales, (0, 1))
        load_rows(nc.scalar, xs_raw, x_scales, (2, 3))
        nc.sync.dma_start(out=xw_raw[:].bitcast(I32), in_=x_words[0].rearrange("p n t -> p (n t)").bitcast(I32))
        load_rows(nc.scalar, ws_raw[0], w1_scales, (0, 1, 2, 3))
        nc.scalar.dma_start(out=gain[:], in_=gn.rearrange("(p t) o -> p (t o)", t=4))
        nc.sync.dma_start(out=seed_sb[0][:], in_=seed_v[:, :, 0:HALF])
        nbr = [load_list("e1_sb", e1), load_list("e2_sb", e2)]
        nc.sync.dma_start(out=seed_sb[1][:], in_=seed_v[:, :, HALF:S])
        with nc.allow_non_contiguous_dma(reason="one value a partition and chunk"):
            nc.sync.dma_start(out=known[:], in_=kn[0, :].rearrange("(c p) -> p c", p=P))
        nc.sync.dma_start(out=ww_raw[1][:].bitcast(I32), in_=w2_words[0].bitcast(I32))
        load_rows(nc.sync, ws_raw[1], w2_scales, (0, 1, 2, 3))
        nc.sync.dma_start(out=ww_raw[2][:].bitcast(I32), in_=w3_words[0].bitcast(I32))
        mv_sb = load_list("mv_sb", mv)
        load_rows(nc.sync, ws_raw[2], w3_scales, (0, 1, 2, 3))
        nc.sync.dma_start(out=res_sb[:], in_=res.rearrange("(p t) j -> p t j", t=4))

        w1w = deal_words("w1w", ww_raw[0], True)
        w1s = deal_scales("w1s", ws_raw[0], nc.gpsimd)
        gain75 = new("gain75", [P, 4], F32)
        nc.scalar.activation(out=gain75[:], in_=gain[:], func=ACT.Copy, scale=0.75)

        xq = [new("xq%d" % h, [P, HALF], U32) for h in range(2)]
        xqs = [new("xqs%d" % h, [P, HALF], U8) for h in range(2)]
        for h in range(2):
            nc.vector.tensor_copy(out=xqs[h][:], in_=xs_raw[:].indirect(entries(offs_sb, HALF * h, HALF)))
            nc.vector.tensor_copy(out=xq[h][:], in_=xw_raw[:].indirect(entries(offs_sb, HALF * h, HALF)))

        unknown = new("unknown", [P, NCH], F32)
        nc.vector.tensor_scalar(out=unknown[:], in0=known[:], scalar1=-1.0, scalar2=1.0, op0=ALU.mult, op1=ALU.add)

        y = [new("y%d" % t, [P, S], F32) for t in range(4)]
        for h in range(2):
            for t in (0, 2, 1, 3):
                bank = psum(4 * (1 - h) + t, [P, HALF])
                product(bank[:], w1w, w1s, t, xq[h][:], xqs[h][:])
                dst = y[t][:, HALF * h : HALF * (h + 1)]
                if t >= 2:
                    nc.vector.tensor_scalar(out=dst, in0=bank[:], scalar1=gain75[:, t : t + 1], scalar2=None, op0=ALU.mult)
                else:
                    nc.scalar.activation(out=dst, in_=bank[:], func=ACT.Copy, scale=gain75[:, t : t + 1])


        picked = [{}, {}]
        h_raw = new("h_raw", [P, 4, S], F32)
        hg = [new("hg%d" % t, [P, S], F32) for t in range(4)]
        held = {}

        def fetch(c):
            for k in range(2):
                picked[k][c] = new("picked%d" % k, [P, 4, CH], F32, bufs=4)
            for t in range(4):
                for k in range(2):
                    gather((k, t) in V_STAGE2[c], picked[k][c][:, t, :], y[t], entries(nbr[k], CH * c, CH))

        def scale_seed(h):
            for t in range(4):
                nc.gpsimd.tensor_scalar(
                    out=seed_gain[h][:, t, :], in0=seed_sb[h][:, t, :], scalar1=gain[:, t : t + 1], scalar2=0.0, op0=ALU.mult, op1=ALU.add
                )

        def known_part(c):
            bank = psum(4 + (c + 1) % 4, [P, 4, P])
            for t in range(4):
                nc.tensor.transpose(bank[:, t, :], seed_gain[c // 2][:, t, CH * (c % 2) : CH * (c % 2 + 1)], ident[:])
            part = new("held%d" % c, [P, 2, P, 2], F32)
            nc.scalar.activation(out=part[:], in_=bank[:].rearrange("j (u e) p -> j u p e", e=2), func=ACT.Copy, scale=known[:, c : c + 1])
            held[c] = part

        turned = {}

        def turn(c):
            bank = psum(c, [P, 4, P])
            turned[c] = bank
            for t in range(4):
                for k in range(2):
                    nc.tensor.matmul(bank[:, t, :], lhsT=picked[k][c][:, t, :], rhs=ident[:], is_transpose=True, start=(k == 0), stop=(k == 1))

        def spread(c):
            bank = turned[c]
            back = psum(4 + (c + 1) % 4, [P, 2, P])
            for u in range(2):
                zt = new("zt%d_%d" % (c, u), [P, 2 * P], BF16)
                nc.vector.scalar_tensor_tensor(
                    out=zt[:].rearrange("j (p e) -> j p e", e=2), in0=bank[:, 2 * u : 2 * u + 2, :].rearrange("j e p -> j p e"),
                    scalar=unknown[:, c : c + 1], in1=held[c][:, u, :, :], op0=ALU.mult, op1=ALU.add,
                )
                nc.tensor.transpose(back[:, u, :], zt[:].bitcast(F32), ident[:])
            z = new("z%d" % c, [P, 4 * CH], BF16)
            copy = nc.vector.tensor_copy if c in [] else nc.scalar.copy
            copy(out=z[:].bitcast(F32).rearrange("p (j u) -> p j u", u=2), in_=back[:].rearrange("p u j -> p j u"))
            return z

        def second_product(c, z):
            codes = new("zc%d" % c, [P, CH], U32)
            scales = new("zs%d" % c, [P, CH], U8)
            nc.vector.quantize_mx(out=codes[:].bitcast(FP8X4), scales=scales[:], in_=z[:])
            if c + 1 < NCH:
                bank = psum(c, [P, 4, CH])
                for t in range(4):
                    product(bank[:, t, :], w2w, w2s, t, codes[:], scales[:])
                nc.scalar.activation(out=h_raw[:, :, CH * c : CH * (c + 1)], in_=bank[:], func=ACT.Tanh)
                return
            for u in (0, 1):
                bank = psum(3 + 2 * u, [P, 2, CH])
                for e in range(2):
                    product(bank[:, e, :], w2w, w2s, 2 * u + e, codes[:], scales[:])
                nc.scalar.activation(out=h_raw[:, 2 * u : 2 * u + 2, CH * c : CH * (c + 1)], in_=bank[:], func=ACT.Tanh)

        def apply_gain(start, stop):
            for t in range(4):
                nc.vector.tensor_scalar(out=hg[t][:, start:stop], in0=h_raw[:, t, start:stop], scalar1=gain[:, t : t + 1], scalar2=None, op0=ALU.mult)

        zs = {}
        seed_gain = [new("seed_gain%d" % h, [P, 4, HALF], F32) for h in range(2)]
        scale_seed(0)
        scale_seed(1)
        w2w = deal_words("w2w", ww_raw[1], False)
        w2s = deal_scales("w2s", ws_raw[1], nc.gpsimd)
        fetch(0)
        fetch(1)
        fetch(2)
        fetch(3)
        known_part(0)
        known_part(1)
        known_part(2)
        known_part(3)
        turn(0)
        turn(1)
        turn(2)
        turn(3)
        zs[0] = spread(0)
        zs[1] = spread(1)
        second_product(0, zs[0])
        zs[2] = spread(2)
        second_product(1, zs[1])
        zs[3] = spread(3)
        second_product(2, zs[2])
        w3w = deal_words("w3w", ww_raw[2], False)
        w3s = deal_scales("w3s", ws_raw[2], nc.gpsimd)
        apply_gain(0, HALF)
        apply_gain(HALF, S - CH)
        second_product(3, zs[3])
        apply_gain(S - CH, S)

        out_v = out_0.rearrange("(p t) j -> p t j", t=4)
        out_codes = new("out_codes", [P, S], U32)
        out_scales = new("out_scales", [P, S], U8)
        words_v = out_1[0].rearrange("p n t -> p (n t)").bitcast(I32)
        moved = {}
        z2 = {}
        result = {}
        sums = {}

        def move(c):
            moved[c] = new("moved", [P, 4, CH], BF16, bufs=4)
            for t in range(4):
                gather(t in V_STAGE3[c], moved[c][:, t, :], hg[t], entries(mv_sb, CH * c, CH))

        def weave(c):
            z2[c] = new("z2_%d" % c, [P, 4 * CH], BF16)
            interleave(c not in S_WEAVE, z2[c], moved[c])

        def third_product(c):
            codes = new("z2c%d" % c, [P, CH], U32)
            scales = new("z2s%d" % c, [P, CH], U8)
            nc.vector.quantize_mx(out=codes[:].bitcast(FP8X4), scales=scales[:], in_=z2[c][:])
            bank = psum(4 + (c + 1) % 4, [P, 4, CH])
            for t in range(4):
                product(bank[:, t, :], w3w, w3s, t, codes[:], scales[:])
            sums[c] = bank

        def add_residual(c):
            bank = sums[c]
            result[c] = new("result%d" % c, [P, 4, CH], F32)
            nc.vector.tensor_tensor(out=result[c][:], in0=bank[:], in1=res_sb[:, :, CH * c : CH * (c + 1)], op=ALU.add)
            nc.sync.dma_start(out=out_v[:, :, CH * c : CH * (c + 1)], in_=result[c][:])

        rounds = {}

        def round_out(c):
            rounds[c] = new("rounded%d" % c, [P, 4 * CH], BF16)
            interleave(c in V_CAST, rounds[c], result[c])

        def hand_on(c):
            rounded = rounds[c]
            cols = slice(CH * c, CH * (c + 1))
            nc.vector.quantize_mx(out=out_codes[:, cols].bitcast(FP8X4), scales=out_scales[:, cols], in_=rounded[:])
            if c % 2 == 1:
                cols = slice(CH * (c - 1), CH * (c + 1))
                nc.sync.dma_start(out=words_v[:, cols], in_=out_codes[:, cols].bitcast(I32))

        move(0)
        move(1)
        move(2)
        move(3)
        weave(0)
        third_product(0)
        weave(1)
        third_product(1)
        add_residual(0)
        weave(2)
        third_product(2)
        add_residual(1)
        weave(3)
        third_product(3)
        add_residual(2)
        add_residual(3)
        round_out(0)
        round_out(1)
        round_out(2)
        round_out(3)
        hand_on(0)
        hand_on(1)
        hand_on(2)
        hand_on(3)
        for q in range(4):
            queue = nc.sync if q % 2 == 0 else nc.scalar
            queue.dma_start(out=out_2[0, 4 * q : 4 * q + 4, :].bitcast(I32), in_=out_scales[32 * q : 32 * q + 4, :].bitcast(I32))
